import numpy as np
import ml_dtypes


def mxq(x, axis, fmt="e4m3"):
    dtype, down = {"e4m3": (ml_dtypes.float8_e4m3fn, 7), "e5m2": (ml_dtypes.float8_e5m2, 14)}[fmt]
    v = np.moveaxis(np.asarray(x, np.float32).astype(ml_dtypes.bfloat16).astype(np.float64), axis, -1)
    blocks = v.reshape(v.shape[:-1] + (-1, 32))
    amax = np.abs(blocks).max(-1, keepdims=True)
    byte = np.maximum(np.where(amax > 0, np.frexp(amax)[1] - 1 + 127, 0) - down, 1)
    scale = np.exp2(byte - 127.0)
    codes = (blocks / scale).astype(np.float32).astype(dtype).astype(np.float64)
    return np.moveaxis((codes * scale).reshape(v.shape), -1, axis)


WIDE = False


def mx_kscale(k):
    if not WIDE:
        return np.ones(k)
    levels = np.array([10, -10, 5, -5, 0])
    if k % 512:
        return np.exp2(np.random.permutation(np.resize(levels, k // 32))).repeat(32)
    a = np.empty((k // 512, 16))
    for p in range(k // 512):
        a[p, :8] = np.random.permutation(np.resize(levels, 8))
        for g in range(8):
            far = levels[np.abs(levels - a[p, g]) >= 10]
            a[p, g + 8] = far[np.random.randint(len(far))]
    return np.exp2(a.ravel()).repeat(32)


def f64(x):
    return np.asarray(x).astype(np.float64)


def striped(idx):
    return np.tile(idx.reshape(-1, 16).T, (8, 1)).astype(np.uint16)


def unstriped(offs):
    return offs[:16].T.reshape(-1).astype(np.int64)


E2M1 = np.array([0.0, 0.5, 1.0, 1.5, 2.0, 3.0, 4.0, 6.0, -0.0, -0.5, -1.0, -1.5, -2.0, -3.0, -4.0, -6.0])


def pack_weight(w, fmt):
    k, n = w.shape
    w = f64(np.asarray(w, np.float32).astype(ml_dtypes.bfloat16)).reshape(k // 32, 32, n)
    amax = np.abs(w).max(1)
    if fmt == "e4m3":
        byte = np.frexp(amax)[1] - 1 + 127 - 7
    else:
        mant, ex = np.frexp(amax / 6.0)
        byte = np.where(mant > 0.5, ex, ex - 1) + 127
    byte = np.clip(np.where(amax > 0, byte, 1), 1, 254)
    scaled = (w * np.exp2(127.0 - byte)[:, None, :]).reshape(k, n).astype(np.float32)
    by_word = np.ascontiguousarray(scaled.reshape(k // 512, 128, 4, n).transpose(0, 1, 3, 2))
    if fmt == "e4m3":
        words = by_word.astype(ml_dtypes.float8_e4m3fn).view(np.uint8)
    else:
        c = by_word.astype(ml_dtypes.float4_e2m1fn).view(np.uint8) & 0xF
        words = (c[..., 0::2] | (c[..., 1::2] << 4)).reshape(k // 512, 128, 2 * n)
    return np.ascontiguousarray(words), np.ascontiguousarray(byte.astype(np.uint8).reshape(k // 512, 16, n))


def unpack_weight(words, scales, fmt):
    g, _, n = scales.shape
    words = np.ascontiguousarray(words).reshape(g, 128, n, -1)
    if fmt == "e4m3":
        vals = words.view(ml_dtypes.float8_e4m3fn).astype(np.float64)
    else:
        nib = np.empty((g, 128, n, 4), np.uint8)
        nib[..., 0::2] = words & 0xF
        nib[..., 1::2] = words >> 4
        vals = E2M1[nib]
    vals = vals * np.repeat(np.exp2(scales.astype(np.float64) - 127.0), 8, axis=1)[..., None]
    return vals.transpose(0, 1, 3, 2).reshape(g * 512, n)


def gelu(v):
    return 0.5 * v * (1.0 + np.tanh(np.sqrt(2.0 / np.pi) * (v + 0.044715 * v**3)))


K, H, N, T, S = 1024, 512, 384, 4096, 1024

def setup_inputs():
    n = np.random.standard_normal
    s = mx_kscale(K)[:, None]
    u = mx_kscale(H)[:, None]
    tab_words, tab_scales = pack_weight(n((K, T)) * s, "e2m1")
    aw = (0.8 * n((K, H)) / np.sqrt(K) / s).astype(np.float32)
    bw_words, bw_scales = pack_weight(0.8 * n((K, H)) / np.sqrt(K) / s, "e4m3")
    gain = (np.exp(0.3 * n(H)) * u[:, 0]).astype(np.float32)
    dw_words, dw_scales = pack_weight(1.5 * n((H, N)) / np.sqrt(H) / u, "e2m1")
    return {"tab_words": tab_words, "tab_scales": tab_scales,
            "offs": striped(np.random.permutation(T)[:S]),
            "offs2": striped(np.random.permutation(T)[:S]),
            "aw": aw, "bw_words": bw_words, "bw_scales": bw_scales,
            "gain": gain, "dw_words": dw_words, "dw_scales": dw_scales}

def reference(tab_words, tab_scales, offs, offs2, aw, bw_words, bw_scales,
              gain, dw_words, dw_scales):
    TW = unpack_weight(tab_words, tab_scales, "e2m1")
    v = TW[:, unstriped(offs)]
    v2 = TW[:, unstriped(offs2)]
    A = mxq(f64(aw), 0, "e4m3")
    B = unpack_weight(bw_words, bw_scales, "e4m3")
    D = unpack_weight(dw_words, dw_scales, "e2m1")
    a_pre = A.T @ v
    a_post = A.T @ v2
    b_pre = B.T @ v
    b_post = B.T @ v2
    d = a_pre * b_post - b_pre * a_post
    h = np.tanh(d) * f64(gain)[:, None]
    hq = mxq(h, 0, "e4m3")
    return D.T @ hq

@@ -1,0 +1,251 @@
+from contextlib import ExitStack
+
+import concourse.mybir as mybir
+
+K, H, N, T, S = 1024, 512, 384, 4096, 1024
+FLOPS = 2 * (4 * K * H * S + H * N * S)
+
+F32 = mybir.dt.float32
+BF16 = mybir.dt.bfloat16
+I32 = mybir.dt.int32
+U32 = mybir.dt.uint32
+U16 = mybir.dt.uint16
+U8 = mybir.dt.uint8
+FP8X4 = mybir.dt.float8_e4m3fn_x4
+FP4X4 = mybir.dt.float4_e2m1fn_x4
+ACT = mybir.ActivationFunctionType
+ALU = mybir.AluOpType
+
+P = 128
+PACK = 4
+PASSES = K // (P * PACK)
+HALF = 512
+HALVES = S // HALF
+CHUNK = 128
+CHUNKS = S // CHUNK
+N_TILES = N // P
+
+
+def tile_list_synapse_direction_evidence_kernel(
+    tc, tab_words, tab_scales, offs, offs2, aw, bw_words, bw_scales, gain, dw_words, dw_scales, out
+):
+    nc = tc.nc
+    with ExitStack() as ctx:
+        lists = ctx.enter_context(tc.tile_pool(name="lists", bufs=1))
+        keep = ctx.enter_context(tc.tile_pool(name="keep", bufs=1))
+        ring = ctx.enter_context(tc.tile_pool(name="ring", bufs=4))
+        psum = ctx.enter_context(tc.psum_pool(name="psum", bufs=8))
+
+        idx = [lists.tile([P, S // 16], U16, name="idx%d" % l) for l in range(2)]
+        nc.sync.dma_start(idx[0][:], offs)
+
+        bw_sc_raw = keep.tile([P, PASSES, H], U8, name="bw_sc_raw", tag="stage1", align_bytes=64)
+        nc.vector.memset(bw_sc_raw[:].bitcast(I32), 0)
+
+        tab_sc = keep.tile([P, T], U8, name="tab_sc", align_bytes=64)
+        for q in range(4):
+            nc.sync.dma_start(
+                tab_sc[32 * q + 24 : 32 * q + 32, :].bitcast(I32), tab_scales[:, 4 * q : 4 * q + 4, :].bitcast(I32)
+            )
+            nc.vector.memset(tab_sc[32 * q : 32 * q + 24, :].bitcast(I32), 0)
+        nc.sync.dma_start(idx[1][:], offs2)
+
+        bw_raw = keep.tile([P, PASSES, H], I32, name="bw_raw", tag="stage0", align_bytes=64)
+        nc.sync.dma_start(bw_raw[:], bw_words.rearrange("a p c i -> p a (c i)").bitcast(I32))
+        tab_w = [keep.tile([P, T], U16, name="tab_w%d" % a, align_bytes=64) for a in range(PASSES)]
+        nc.sync.dma_start(tab_w[0][:].bitcast(I32), tab_words[0].bitcast(I32))
+        for q in range(4):
+            nc.sync.dma_start(
+                bw_sc_raw[32 * q : 32 * q + 4].bitcast(I32),
+                bw_scales[:, 4 * q : 4 * q + 4, :].rearrange("a r c -> r a c").bitcast(I32),
+            )
+        nc.sync.dma_start(tab_w[1][:].bitcast(I32), tab_words[1].bitcast(I32))
+
+        v_sc = {}
+        for h in range(HALVES):
+            for a in range(PASSES):
+                v_sc[a, h] = keep.tile([P, 2 * HALF], U8, name="v_sc%d_%d" % (a, h), align_bytes=64)
+                nc.gpsimd.memset(v_sc[a, h][96:128, :].bitcast(I32), 0)
+        dw_sc = keep.tile([P, N], U8, name="dw_sc", align_bytes=64)
+        nc.gpsimd.memset(dw_sc[:].bitcast(I32), 0)
+        for q in range(4):
+            nc.gpsimd.dma_start(
+                dw_sc[32 * q : 32 * q + 4, :].bitcast(I32), dw_scales[0, 4 * q : 4 * q + 4, :].bitcast(I32)
+            )
+        dw_w = keep.tile([P, 2 * N], U8, name="dw_w", align_bytes=64)
+        nc.gpsimd.dma_start(dw_w[:].bitcast(I32), dw_words[0].bitcast(I32))
+        gain_sb = keep.tile([P, PACK], F32, name="gain_sb", align_bytes=64)
+        nc.gpsimd.dma_start(gain_sb[:], gain.rearrange("(p t) -> p t", t=PACK))
+
+        warm_in = keep.tile([P, 1], F32, name="warm_in")
+        warm_out = keep.tile([P, 1], F32, name="warm_out")
+        nc.vector.memset(warm_in[:], 0.0)
+        nc.scalar.activation(warm_out[:], warm_in[:], ACT.Tanh)
+
+        def offsets(l, h):
+            return idx[l][:, h * (HALF // 16) : (h + 1) * (HALF // 16)]
+
+        v_w = {}
+
+        def gather_scales(h, queue):
+            both = keep.tile([P, 2 * HALF], U8, name="v_sc_both", align_bytes=64)
+            for l in range(2):
+                nc.vector.tensor_copy(both[:, l * HALF : (l + 1) * HALF], tab_sc[:].indirect(offsets(l, h)))
+            for a in range(PASSES):
+                first = 24 + 4 * a
+                queue.dma_start(v_sc[a, h][0:100, :].bitcast(I32), both[first : first + 100, :].bitcast(I32))
+
+        def gather_words(a, l, h):
+            nc.vector.tensor_copy(v_w[a, h][:, l * HALF : (l + 1) * HALF], tab_w[a][:].indirect(offsets(l, h)))
+
+        weights = {}
+
+        def first_stage_pass(dst, role, t, a, l, j0, width):
+            codes, scales = weights[role, a]
+            h, c0 = divmod(j0, HALF)
+            nc.tensor.matmul_mx(
+                out=dst,
+                lhsT=codes[:, t * P : (t + 1) * P].bitcast(FP8X4),
+                lhsT_scale=scales[:, t * P : (t + 1) * P],
+                rhs=v_w[a, h][:, l * HALF + c0 : l * HALF + c0 + width].bitcast(FP4X4),
+                rhs_scale=v_sc[a, h][:, l * HALF + c0 : l * HALF + c0 + width],
+                start=(a == 0),
+                stop=(a == PASSES - 1),
+            )
+
+        gather_scales(0, nc.sync)
+
+        bw_q = keep.tile([P, PASSES, H], I32, name="bw_q", align_bytes=64)
+        nc.vector.tensor_copy(
+            bw_q[:].rearrange("p a (t c i) -> p a c t i", t=4, i=4),
+            bw_raw[:].rearrange("p a (c i t) -> p a c t i", t=4, i=4),
+        )
+        bw_sc = keep.tile([P, PASSES, H], U8, name="bw_sc", align_bytes=64)
+        nc.vector.tensor_copy(
+            bw_sc[:].rearrange("p a (t m) -> p a t m", t=4),
+            bw_sc_raw[:].rearrange("p a (m t) -> p a t m", t=4),
+        )
+
+        aw_raw = []
+        for a in range(PASSES):
+            raw = keep.tile([P, PACK, H], F32, name="aw_raw%d" % a, tag="stage%d" % a, align_bytes=64)
+            nc.sync.dma_start(raw[:], aw[512 * a : 512 * (a + 1), :].rearrange("(p i) c -> p i c", i=PACK))
+            aw_raw.append(raw)
+
+        aw_bf = []
+        for a in range(PASSES):
+            weights["b", a] = (bw_q[:, a, :], bw_sc[:, a, :])
+            grouped = keep.tile([P, PACK * H], BF16, name="aw_bf%d" % a, tag="aw_bf%d" % a, align_bytes=64)
+            nc.scalar.copy(
+                grouped[:].rearrange("p (t m i) -> p m t i", t=4, i=4),
+                aw_raw[a][:].rearrange("p i (m t) -> p m t i", t=4),
+            )
+            aw_bf.append(grouped)
+
+        banks = {}
+        for a in range(PASSES):
+            v_w[a, 0] = keep.tile([P, 2 * HALF], U16, name="v_w%d_0" % a, align_bytes=64)
+            for l in range(2):
+                gather_words(a, l, 0)
+                for t in range(PACK):
+                    if a == 0:
+                        banks[l, t] = psum.tile([P, HALF], F32, name="bank", tag="bank")
+                    first_stage_pass(banks[l, t][:], "b", t, a, l, 0, HALF)
+        b0 = keep.tile([P, 2, PACK, HALF], F32, name="b0", tag="stage1", align_bytes=64)
+        for t in range(PACK):
+            for l in range(2):
+                nc.scalar.copy(b0[:, l, t, :], banks[l, t][:])
+
+        gather_scales(1, nc.sync)
+        for a in range(PASSES):
+            codes = keep.tile([P, H], U32, name="aw_q%d" % a, align_bytes=64)
+            scales = keep.tile([P, H], U8, name="aw_sc%d" % a, align_bytes=64)
+            nc.vector.quantize_mx(out=codes[:].bitcast(FP8X4), scales=scales[:], in_=aw_bf[a][:])
+            weights["a", a] = (codes[:], scales[:])
+            v_w[a, 1] = keep.tile(
+                [P, 2 * HALF], U16, name="v_w%d_1" % a, tag=("stage0", "aw_bf1")[a], align_bytes=64
+            )
+            for l in range(2):
+                gather_words(a, l, 1)
+
+        out_v = out.rearrange("(c p) j -> p c j", p=P)
+
+        def combine(a_banks, b_vals, diff, engine):
+            prods = []
+            for l in range(2):
+                prod = ring.tile(list(diff.shape), F32, name="prod%d" % l, align_bytes=64)
+                nc.vector.tensor_tensor(prod[:], a_banks[l], b_vals[1 - l], ALU.mult)
+                prods.append(prod)
+            engine.tensor_tensor(diff, prods[0][:], prods[1][:], ALU.subtract)
+
+        def squash(diff, width):
+            th = ring.tile([P, width, PACK], F32, name="th", align_bytes=64)
+            nc.scalar.activation(
+                th[:].rearrange("p (c i) t -> p c t i", i=4),
+                diff.rearrange("p t (c i) -> p c t i", i=4),
+                ACT.Tanh,
+            )
+            return th
+
+        def scale(th, width):
+            hb = ring.tile([P, width, PACK], BF16, name="hb", align_bytes=64)
+            nc.vector.tensor_tensor(
+                hb[:], th[:], gain_sb[:].unsqueeze(1).to_broadcast([P, width, PACK]), ALU.mult
+            )
+            return hb
+
+        def second_stage(hb, j0, width):
+            codes = ring.tile([P, width], U32, name="h_q", align_bytes=64)
+            scales = ring.tile([P, width], U8, name="h_sc", align_bytes=64)
+            nc.vector.quantize_mx(
+                out=codes[:].bitcast(FP8X4), scales=scales[:], in_=hb[:].rearrange("p j t -> p (j t)")
+            )
+            res = ring.tile([P, N_TILES, width], F32, name="res", align_bytes=64)
+            for c0 in range(0, width, CHUNK):
+                bank = psum.tile([P, N_TILES, CHUNK], F32, name="bank", tag="bank")
+                for n in range(N_TILES):
+                    nc.tensor.matmul_mx(
+                        out=bank[:, n, :],
+                        lhsT=dw_w[:, 2 * P * n : 2 * P * (n + 1)].bitcast(FP4X4),
+                        lhsT_scale=dw_sc[:, P * n : P * (n + 1)],
+                        rhs=codes[:, c0 : c0 + CHUNK].bitcast(FP8X4),
+                        rhs_scale=scales[:, c0 : c0 + CHUNK],
+                        start=True,
+                        stop=True,
+                    )
+                nc.scalar.copy(res[:, :, c0 : c0 + CHUNK], bank[:])
+            nc.sync.dma_start(out_v[:, :, j0 : j0 + width], res[:])
+
+        b1 = keep.tile([P, 2, PACK, HALF], F32, name="b1", align_bytes=64)
+        b_all = [b0, b1]
+        ths = {}
+        hbs = {}
+        for step in range(CHUNKS + 3):
+            if step < CHUNKS:
+                j0 = step * CHUNK
+                h, c0 = divmod(j0, HALF)
+                a_banks = []
+                for l in range(2):
+                    bank = psum.tile([P, PACK, CHUNK], F32, name="bank", tag="bank")
+                    for t in range(PACK):
+                        for a in range(PASSES):
+                            first_stage_pass(bank[:, t, :], "a", t, a, l, j0, CHUNK)
+                    a_banks.append(bank[:])
+                diff = ring.tile([P, PACK, CHUNK], F32, name="diff", align_bytes=64)
+                combine(
+                    a_banks,
+                    [b_all[h][:, l, :, c0 : c0 + CHUNK] for l in range(2)],
+                    diff[:],
+                    nc.vector if step == CHUNKS - 1 else nc.gpsimd,
+                )
+                ths[step] = squash(diff[:], CHUNK)
+            if step < PACK:
+                for l in range(2):
+                    bank = psum.tile([P, HALF], F32, name="bank", tag="bank")
+                    for a in range(PASSES):
+                        first_stage_pass(bank[:], "b", step, a, l, HALF, HALF)
+                    nc.scalar.copy(b1[:, l, step, :], bank[:])
+            if 2 <= step < CHUNKS + 2:
+                hbs[step - 2] = scale(ths[step - 2], CHUNK)
+            if step >= 3:
+                second_stage(hbs[step - 3], (step - 3) * CHUNK, CHUNK)

@@ -42,7 +42,7 @@ def tile_list_synapse_direction_evidence_kernel(
         bw_sc_raw = keep.tile([P, PASSES, H], U8, name="bw_sc_raw", tag="stage1", align_bytes=64)
         nc.vector.memset(bw_sc_raw[:].bitcast(I32), 0)
 
-        tab_sc = keep.tile([P, T], U8, name="tab_sc", align_bytes=64)
+        tab_sc = keep.tile([P, T], U8, name="tab_sc", tag="tab_sc", align_bytes=64)
         for q in range(4):
             nc.sync.dma_start(
                 tab_sc[32 * q + 24 : 32 * q + 32, :].bitcast(I32), tab_scales[:, 4 * q : 4 * q + 4, :].bitcast(I32)
@@ -66,16 +66,8 @@ def tile_list_synapse_direction_evidence_kernel(
             for a in range(PASSES):
                 v_sc[a, h] = keep.tile([P, 2 * HALF], U8, name="v_sc%d_%d" % (a, h), align_bytes=64)
                 nc.gpsimd.memset(v_sc[a, h][96:128, :].bitcast(I32), 0)
-        dw_sc = keep.tile([P, N], U8, name="dw_sc", align_bytes=64)
-        nc.gpsimd.memset(dw_sc[:].bitcast(I32), 0)
-        for q in range(4):
-            nc.gpsimd.dma_start(
-                dw_sc[32 * q : 32 * q + 4, :].bitcast(I32), dw_scales[0, 4 * q : 4 * q + 4, :].bitcast(I32)
-            )
-        dw_w = keep.tile([P, 2 * N], U8, name="dw_w", align_bytes=64)
-        nc.gpsimd.dma_start(dw_w[:].bitcast(I32), dw_words[0].bitcast(I32))
         gain_sb = keep.tile([P, PACK], F32, name="gain_sb", align_bytes=64)
-        nc.gpsimd.dma_start(gain_sb[:], gain.rearrange("(p t) -> p t", t=PACK))
+        nc.sync.dma_start(gain_sb[:], gain.rearrange("(p t) -> p t", t=PACK))
 
         warm_in = keep.tile([P, 1], F32, name="warm_in")
         warm_out = keep.tile([P, 1], F32, name="warm_out")
@@ -88,7 +80,7 @@ def tile_list_synapse_direction_evidence_kernel(
         v_w = {}
 
         def gather_scales(h, queue):
-            both = keep.tile([P, 2 * HALF], U8, name="v_sc_both", align_bytes=64)
+            both = keep.tile([P, 2 * HALF], U8, name="v_sc_both", tag="both", align_bytes=64)
             for l in range(2):
                 nc.vector.tensor_copy(both[:, l * HALF : (l + 1) * HALF], tab_sc[:].indirect(offsets(l, h)))
             for a in range(PASSES):
@@ -142,19 +134,29 @@ def tile_list_synapse_direction_evidence_kernel(
             )
             aw_bf.append(grouped)
 
-        banks = {}
         for a in range(PASSES):
             v_w[a, 0] = keep.tile([P, 2 * HALF], U16, name="v_w%d_0" % a, align_bytes=64)
             for l in range(2):
                 gather_words(a, l, 0)
-                for t in range(PACK):
-                    if a == 0:
-                        banks[l, t] = psum.tile([P, HALF], F32, name="bank", tag="bank")
-                    first_stage_pass(banks[l, t][:], "b", t, a, l, 0, HALF)
-        b0 = keep.tile([P, 2, PACK, HALF], F32, name="b0", tag="stage1", align_bytes=64)
-        for t in range(PACK):
+
+        def chunk_products(role, l, j0):
+            bank = psum.tile([P, PACK, CHUNK], F32, name="bank", tag="bank")
+            for t in range(PACK):
+                for a in range(PASSES):
+                    first_stage_pass(bank[:, t, :], role, t, a, l, j0, CHUNK)
+            return bank[:].rearrange("p t j -> p j t")
+
+        per_half = HALF // CHUNK
+        b0 = keep.tile([P, per_half, 2, CHUNK, PACK], F32, name="b0", tag="stage1", align_bytes=64)
+        b1 = keep.tile([P, per_half, 2, CHUNK, PACK], F32, name="b1", align_bytes=64)
+        b_all = [b0, b1]
+
+        def b_products(c):
             for l in range(2):
-                nc.scalar.copy(b0[:, l, t, :], banks[l, t][:])
+                nc.scalar.copy(b_all[c // per_half][:, c % per_half, l], chunk_products("b", l, c * CHUNK))
+
+        for c in range(per_half):
+            b_products(c)
 
         gather_scales(1, nc.sync)
         for a in range(PASSES):
@@ -168,6 +170,15 @@ def tile_list_synapse_direction_evidence_kernel(
             for l in range(2):
                 gather_words(a, l, 1)
 
+        dw_w = keep.tile([P, 2 * N], U8, name="dw_w", tag="tab_sc", align_bytes=64)
+        nc.sync.dma_start(dw_w[:].bitcast(I32), dw_words[0].bitcast(I32))
+        dw_sc = keep.tile([P, N], U8, name="dw_sc", tag="both", align_bytes=64)
+        nc.vector.memset(dw_sc[:].bitcast(I32), 0)
+        for q in range(4):
+            nc.sync.dma_start(
+                dw_sc[32 * q : 32 * q + 4, :].bitcast(I32), dw_scales[0, 4 * q : 4 * q + 4, :].bitcast(I32)
+            )
+
         out_v = out.rearrange("(c p) j -> p c j", p=P)
 
         def combine(a_banks, b_vals, diff, engine):
@@ -180,11 +191,7 @@ def tile_list_synapse_direction_evidence_kernel(
 
         def squash(diff, width):
             th = ring.tile([P, width, PACK], F32, name="th", align_bytes=64)
-            nc.scalar.activation(
-                th[:].rearrange("p (c i) t -> p c t i", i=4),
-                diff.rearrange("p t (c i) -> p c t i", i=4),
-                ACT.Tanh,
-            )
+            nc.scalar.activation(th[:], diff, ACT.Tanh)
             return th
 
         def scale(th, width):
@@ -216,35 +223,21 @@ def tile_list_synapse_direction_evidence_kernel(
                 nc.scalar.copy(res[:, :, c0 : c0 + CHUNK], bank[:])
             nc.sync.dma_start(out_v[:, :, j0 : j0 + width], res[:])
 
-        b1 = keep.tile([P, 2, PACK, HALF], F32, name="b1", align_bytes=64)
-        b_all = [b0, b1]
         ths = {}
         hbs = {}
         for step in range(CHUNKS + 3):
             if step < CHUNKS:
-                j0 = step * CHUNK
-                h, c0 = divmod(j0, HALF)
-                a_banks = []
-                for l in range(2):
-                    bank = psum.tile([P, PACK, CHUNK], F32, name="bank", tag="bank")
-                    for t in range(PACK):
-                        for a in range(PASSES):
-                            first_stage_pass(bank[:, t, :], "a", t, a, l, j0, CHUNK)
-                    a_banks.append(bank[:])
-                diff = ring.tile([P, PACK, CHUNK], F32, name="diff", align_bytes=64)
+                a_banks = [chunk_products("a", l, step * CHUNK) for l in range(2)]
+                diff = ring.tile([P, CHUNK, PACK], F32, name="diff", align_bytes=64)
                 combine(
                     a_banks,
-                    [b_all[h][:, l, :, c0 : c0 + CHUNK] for l in range(2)],
+                    [b_all[step // per_half][:, step % per_half, l] for l in range(2)],
                     diff[:],
                     nc.vector if step == CHUNKS - 1 else nc.gpsimd,
                 )
                 ths[step] = squash(diff[:], CHUNK)
-            if step < PACK:
-                for l in range(2):
-                    bank = psum.tile([P, HALF], F32, name="bank", tag="bank")
-                    for a in range(PASSES):
-                        first_stage_pass(bank[:], "b", step, a, l, HALF, HALF)
-                    nc.scalar.copy(b1[:, l, step, :], bank[:])
+            if step < per_half:
+                b_products(step + per_half)
             if 2 <= step < CHUNKS + 2:
                 hbs[step - 2] = scale(ths[step - 2], CHUNK)
             if step >= 3:

@@ -20,9 +20,9 @@ P = 128
 PACK = 4
 PASSES = K // (P * PACK)
 HALF = 512
-HALVES = S // HALF
 CHUNK = 128
 CHUNKS = S // CHUNK
+PER_HALF = HALF // CHUNK
 N_TILES = N // P
 
 
@@ -39,10 +39,10 @@ def tile_list_synapse_direction_evidence_kernel(
         idx = [lists.tile([P, S // 16], U16, name="idx%d" % l) for l in range(2)]
         nc.sync.dma_start(idx[0][:], offs)
 
-        bw_sc_raw = keep.tile([P, PASSES, H], U8, name="bw_sc_raw", tag="stage1", align_bytes=64)
+        bw_sc_raw = keep.tile([P, PASSES, H], U8, name="bw_sc_raw", align_bytes=64)
         nc.vector.memset(bw_sc_raw[:].bitcast(I32), 0)
 
-        tab_sc = keep.tile([P, T], U8, name="tab_sc", tag="tab_sc", align_bytes=64)
+        tab_sc = keep.tile([P, T], U8, name="tab_sc", tag="table", align_bytes=64)
         for q in range(4):
             nc.sync.dma_start(
                 tab_sc[32 * q + 24 : 32 * q + 32, :].bitcast(I32), tab_scales[:, 4 * q : 4 * q + 4, :].bitcast(I32)
@@ -50,62 +50,44 @@ def tile_list_synapse_direction_evidence_kernel(
             nc.vector.memset(tab_sc[32 * q : 32 * q + 24, :].bitcast(I32), 0)
         nc.sync.dma_start(idx[1][:], offs2)
 
-        bw_raw = keep.tile([P, PASSES, H], I32, name="bw_raw", tag="stage0", align_bytes=64)
+        aw_raw = [keep.tile([P, PACK, H], F32, name="aw_raw%d" % a, align_bytes=64) for a in range(PASSES)]
+
+        def load_aw(a):
+            nc.sync.dma_start(
+                aw_raw[a][:], aw[512 * a : 512 * (a + 1), :].rearrange("(p i) c -> p i c", i=PACK)
+            )
+
+        load_aw(0)
+        bw_raw = keep.tile([P, PASSES, H], I32, name="bw_raw", align_bytes=64)
         nc.sync.dma_start(bw_raw[:], bw_words.rearrange("a p c i -> p a (c i)").bitcast(I32))
-        tab_w = [keep.tile([P, T], U16, name="tab_w%d" % a, align_bytes=64) for a in range(PASSES)]
-        nc.sync.dma_start(tab_w[0][:].bitcast(I32), tab_words[0].bitcast(I32))
         for q in range(4):
             nc.sync.dma_start(
                 bw_sc_raw[32 * q : 32 * q + 4].bitcast(I32),
                 bw_scales[:, 4 * q : 4 * q + 4, :].rearrange("a r c -> r a c").bitcast(I32),
             )
-        nc.sync.dma_start(tab_w[1][:].bitcast(I32), tab_words[1].bitcast(I32))
-
-        v_sc = {}
-        for h in range(HALVES):
-            for a in range(PASSES):
-                v_sc[a, h] = keep.tile([P, 2 * HALF], U8, name="v_sc%d_%d" % (a, h), align_bytes=64)
-                nc.gpsimd.memset(v_sc[a, h][96:128, :].bitcast(I32), 0)
+        tab_w = [keep.tile([P, T], U16, name="tab_w0", align_bytes=64)]
+        nc.sync.dma_start(tab_w[0][:].bitcast(I32), tab_words[0].bitcast(I32))
+        load_aw(1)
         gain_sb = keep.tile([P, PACK], F32, name="gain_sb", align_bytes=64)
         nc.sync.dma_start(gain_sb[:], gain.rearrange("(p t) -> p t", t=PACK))
+
+        v_sc = []
+        for a in range(PASSES):
+            v_sc.append(keep.tile([P, 2 * S], U8, name="v_sc%d" % a, align_bytes=64))
+            nc.gpsimd.memset(v_sc[a][96:128, :].bitcast(I32), 0)
 
         warm_in = keep.tile([P, 1], F32, name="warm_in")
         warm_out = keep.tile([P, 1], F32, name="warm_out")
         nc.vector.memset(warm_in[:], 0.0)
         nc.scalar.activation(warm_out[:], warm_in[:], ACT.Tanh)
 
-        def offsets(l, h):
-            return idx[l][:, h * (HALF // 16) : (h + 1) * (HALF // 16)]
-
-        v_w = {}
-
-        def gather_scales(h, queue):
-            both = keep.tile([P, 2 * HALF], U8, name="v_sc_both", tag="both", align_bytes=64)
-            for l in range(2):
-                nc.vector.tensor_copy(both[:, l * HALF : (l + 1) * HALF], tab_sc[:].indirect(offsets(l, h)))
-            for a in range(PASSES):
-                first = 24 + 4 * a
-                queue.dma_start(v_sc[a, h][0:100, :].bitcast(I32), both[first : first + 100, :].bitcast(I32))
-
-        def gather_words(a, l, h):
-            nc.vector.tensor_copy(v_w[a, h][:, l * HALF : (l + 1) * HALF], tab_w[a][:].indirect(offsets(l, h)))
-
-        weights = {}
-
-        def first_stage_pass(dst, role, t, a, l, j0, width):
-            codes, scales = weights[role, a]
-            h, c0 = divmod(j0, HALF)
-            nc.tensor.matmul_mx(
-                out=dst,
-                lhsT=codes[:, t * P : (t + 1) * P].bitcast(FP8X4),
-                lhsT_scale=scales[:, t * P : (t + 1) * P],
-                rhs=v_w[a, h][:, l * HALF + c0 : l * HALF + c0 + width].bitcast(FP4X4),
-                rhs_scale=v_sc[a, h][:, l * HALF + c0 : l * HALF + c0 + width],
-                start=(a == 0),
-                stop=(a == PASSES - 1),
-            )
-
-        gather_scales(0, nc.sync)
+        both = keep.tile([P, 2 * S], U8, name="v_sc_both", tag="both", align_bytes=64)
+        for l in range(2):
+            nc.vector.tensor_copy(both[:, l * S : (l + 1) * S], tab_sc[:].indirect(idx[l][:]))
+        nc.sync.dma_start(v_sc[0][0:100, :].bitcast(I32), both[24:124, :].bitcast(I32))
+        tab_w.append(keep.tile([P, T], U16, name="tab_w1", tag="table", align_bytes=64))
+        nc.sync.dma_start(tab_w[1][:].bitcast(I32), tab_words[1].bitcast(I32))
+        nc.sync.dma_start(v_sc[1][0:100, :].bitcast(I32), both[28:128, :].bitcast(I32))
 
         bw_q = keep.tile([P, PASSES, H], I32, name="bw_q", align_bytes=64)
         nc.vector.tensor_copy(
@@ -118,59 +100,31 @@ def tile_list_synapse_direction_evidence_kernel(
             bw_sc_raw[:].rearrange("p a (m t) -> p a t m", t=4),
         )
 
-        aw_raw = []
-        for a in range(PASSES):
-            raw = keep.tile([P, PACK, H], F32, name="aw_raw%d" % a, tag="stage%d" % a, align_bytes=64)
-            nc.sync.dma_start(raw[:], aw[512 * a : 512 * (a + 1), :].rearrange("(p i) c -> p i c", i=PACK))
-            aw_raw.append(raw)
+        v_w = {}
 
-        aw_bf = []
+        def gather_words(a, l, h, tag):
+            words = keep.tile([P, HALF], U16, name="v_w%d_%d_%d" % (a, l, h), tag=tag, align_bytes=64)
+            offsets = idx[l][:, h * (HALF // 16) : (h + 1) * (HALF // 16)]
+            nc.vector.tensor_copy(words[:], tab_w[a][:].indirect(offsets))
+            v_w[a, l, h] = words
+
+        weights = {}
         for a in range(PASSES):
-            weights["b", a] = (bw_q[:, a, :], bw_sc[:, a, :])
             grouped = keep.tile([P, PACK * H], BF16, name="aw_bf%d" % a, tag="aw_bf%d" % a, align_bytes=64)
             nc.scalar.copy(
                 grouped[:].rearrange("p (t m i) -> p m t i", t=4, i=4),
                 aw_raw[a][:].rearrange("p i (m t) -> p m t i", t=4),
             )
-            aw_bf.append(grouped)
-
-        for a in range(PASSES):
-            v_w[a, 0] = keep.tile([P, 2 * HALF], U16, name="v_w%d_0" % a, align_bytes=64)
             for l in range(2):
-                gather_words(a, l, 0)
-
-        def chunk_products(role, l, j0):
-            bank = psum.tile([P, PACK, CHUNK], F32, name="bank", tag="bank")
-            for t in range(PACK):
-                for a in range(PASSES):
-                    first_stage_pass(bank[:, t, :], role, t, a, l, j0, CHUNK)
-            return bank[:].rearrange("p t j -> p j t")
-
-        per_half = HALF // CHUNK
-        b0 = keep.tile([P, per_half, 2, CHUNK, PACK], F32, name="b0", tag="stage1", align_bytes=64)
-        b1 = keep.tile([P, per_half, 2, CHUNK, PACK], F32, name="b1", align_bytes=64)
-        b_all = [b0, b1]
-
-        def b_products(c):
-            for l in range(2):
-                nc.scalar.copy(b_all[c // per_half][:, c % per_half, l], chunk_products("b", l, c * CHUNK))
-
-        for c in range(per_half):
-            b_products(c)
-
-        gather_scales(1, nc.sync)
-        for a in range(PASSES):
+                gather_words(a, l, 0, "v_w%d_%d_0" % (a, l))
             codes = keep.tile([P, H], U32, name="aw_q%d" % a, align_bytes=64)
             scales = keep.tile([P, H], U8, name="aw_sc%d" % a, align_bytes=64)
-            nc.vector.quantize_mx(out=codes[:].bitcast(FP8X4), scales=scales[:], in_=aw_bf[a][:])
+            nc.vector.quantize_mx(out=codes[:].bitcast(FP8X4), scales=scales[:], in_=grouped[:])
             weights["a", a] = (codes[:], scales[:])
-            v_w[a, 1] = keep.tile(
-                [P, 2 * HALF], U16, name="v_w%d_1" % a, tag=("stage0", "aw_bf1")[a], align_bytes=64
-            )
-            for l in range(2):
-                gather_words(a, l, 1)
+            weights["b", a] = (bw_q[:, a, :], bw_sc[:, a, :])
+        gather_words(0, 0, 1, "aw_bf1")
 
-        dw_w = keep.tile([P, 2 * N], U8, name="dw_w", tag="tab_sc", align_bytes=64)
+        dw_w = keep.tile([P, 2 * N], U8, name="dw_w", tag="aw_bf0", align_bytes=64)
         nc.sync.dma_start(dw_w[:].bitcast(I32), dw_words[0].bitcast(I32))
         dw_sc = keep.tile([P, N], U8, name="dw_sc", tag="both", align_bytes=64)
         nc.vector.memset(dw_sc[:].bitcast(I32), 0)
@@ -179,30 +133,60 @@ def tile_list_synapse_direction_evidence_kernel(
                 dw_sc[32 * q : 32 * q + 4, :].bitcast(I32), dw_scales[0, 4 * q : 4 * q + 4, :].bitcast(I32)
             )
 
-        out_v = out.rearrange("(c p) j -> p c j", p=P)
+        def passes(bank, role, l, c, a):
+            codes, scales = weights[role, a]
+            h, c0 = divmod(c * CHUNK, HALF)
+            j0 = l * S + c * CHUNK
+            for t in range(PACK):
+                nc.tensor.matmul_mx(
+                    out=bank[:, t, :],
+                    lhsT=codes[:, t * P : (t + 1) * P].bitcast(FP8X4),
+                    lhsT_scale=scales[:, t * P : (t + 1) * P],
+                    rhs=v_w[a, l, h][:, c0 : c0 + CHUNK].bitcast(FP4X4),
+                    rhs_scale=v_sc[a][:, j0 : j0 + CHUNK],
+                    start=(a == 0 and t == 0),
+                    stop=(a == PASSES - 1 and t == PACK - 1),
+                )
 
-        def combine(a_banks, b_vals, diff, engine):
+        products = [("b", 0), ("a", 0), ("b", 1), ("a", 1)]
+        banks = {}
+
+        def open_chunk(c):
+            for role, l in products:
+                banks[role, l, c] = psum.tile([P, PACK, CHUNK], F32, name="bank", tag="bank")
+                passes(banks[role, l, c], role, l, c, 0)
+
+        def cross_products(c):
+            b_vals = keep.tile([P, 2, CHUNK, PACK], F32, name="b%d" % c, tag="b%d" % c, align_bytes=64)
+            for role, l in products:
+                if (role, l, c) not in banks:
+                    banks[role, l, c] = psum.tile([P, PACK, CHUNK], F32, name="bank", tag="bank")
+                    passes(banks[role, l, c], role, l, c, 0)
+                passes(banks[role, l, c], role, l, c, 1)
+                if role == "b":
+                    nc.scalar.copy(b_vals[:, l], banks[role, l, c][:].rearrange("p t j -> p j t"))
             prods = []
             for l in range(2):
-                prod = ring.tile(list(diff.shape), F32, name="prod%d" % l, align_bytes=64)
-                nc.vector.tensor_tensor(prod[:], a_banks[l], b_vals[1 - l], ALU.mult)
+                prod = ring.tile([P, CHUNK, PACK], F32, name="prod%d" % l, align_bytes=64)
+                nc.vector.tensor_tensor(
+                    prod[:], banks["a", l, c][:].rearrange("p t j -> p j t"), b_vals[:, 1 - l], ALU.mult
+                )
                 prods.append(prod)
-            engine.tensor_tensor(diff, prods[0][:], prods[1][:], ALU.subtract)
+            return prods
 
-        def squash(diff, width):
-            th = ring.tile([P, width, PACK], F32, name="th", align_bytes=64)
-            nc.scalar.activation(th[:], diff, ACT.Tanh)
+        def squash(prods, engine):
+            diff = ring.tile([P, CHUNK, PACK], F32, name="diff", align_bytes=64)
+            engine.tensor_tensor(diff[:], prods[0][:], prods[1][:], ALU.subtract)
+            th = ring.tile([P, CHUNK, PACK], F32, name="th", align_bytes=64)
+            nc.scalar.activation(th[:], diff[:], ACT.Tanh)
             return th
 
-        def scale(th, width):
-            hb = ring.tile([P, width, PACK], BF16, name="hb", align_bytes=64)
-            nc.vector.tensor_tensor(
-                hb[:], th[:], gain_sb[:].unsqueeze(1).to_broadcast([P, width, PACK]), ALU.mult
-            )
-            return hb
+        def scale(hb, th, engine):
+            engine.tensor_tensor(hb, th[:], gain_sb[:].unsqueeze(1).to_broadcast([P, CHUNK, PACK]), ALU.mult)
 
-        def second_stage(hb, j0, width):
-            codes = ring.tile([P, width], U32, name="h_q", align_bytes=64)
+        out_v = out.rearrange("(c p) j -> p c j", p=P)
+
+        def second_stage(hb, codes, j0, width):
             scales = ring.tile([P, width], U8, name="h_sc", align_bytes=64)
             nc.vector.quantize_mx(
                 out=codes[:].bitcast(FP8X4), scales=scales[:], in_=hb[:].rearrange("p j t -> p (j t)")
@@ -223,22 +207,34 @@ def tile_list_synapse_direction_evidence_kernel(
                 nc.scalar.copy(res[:, :, c0 : c0 + CHUNK], bank[:])
             nc.sync.dma_start(out_v[:, :, j0 : j0 + width], res[:])
 
+        late = [(0, 1), (1, 0), (1, 1)]
+        hb_first = keep.tile([P, HALF, PACK], BF16, name="hb_first", align_bytes=64)
         ths = {}
         hbs = {}
+        open_chunk(0)
+        open_chunk(1)
         for step in range(CHUNKS + 3):
             if step < CHUNKS:
-                a_banks = [chunk_products("a", l, step * CHUNK) for l in range(2)]
-                diff = ring.tile([P, CHUNK, PACK], F32, name="diff", align_bytes=64)
-                combine(
-                    a_banks,
-                    [b_all[step // per_half][:, step % per_half, l] for l in range(2)],
-                    diff[:],
-                    nc.vector if step == CHUNKS - 1 else nc.gpsimd,
-                )
-                ths[step] = squash(diff[:], CHUNK)
-            if step < per_half:
-                b_products(step + per_half)
-            if 2 <= step < CHUNKS + 2:
-                hbs[step - 2] = scale(ths[step - 2], CHUNK)
-            if step >= 3:
-                second_stage(hbs[step - 3], (step - 3) * CHUNK, CHUNK)
+                prods = cross_products(step)
+            if step < PER_HALF:
+                ths[step] = squash(prods, nc.gpsimd)
+            if step < len(late):
+                gather_words(late[step][0], late[step][1], 1, "b%d" % step)
+            c = step - 1
+            if 0 <= c < PER_HALF - 1:
+                scale(hb_first[:, c * CHUNK : (c + 1) * CHUNK, :], ths[c], nc.gpsimd)
+            c = step - 2
+            if c == PER_HALF - 1:
+                scale(hb_first[:, c * CHUNK : (c + 1) * CHUNK, :], ths[c], nc.vector)
+            if PER_HALF <= c < CHUNKS:
+                hbs[c] = ring.tile([P, CHUNK, PACK], BF16, name="hb", align_bytes=64)
+                scale(hbs[c][:], ths[c], nc.vector)
+            if PER_HALF <= step < CHUNKS:
+                ths[step] = squash(prods, nc.vector)
+            c = step - 3
+            if c == PER_HALF - 1:
+                codes = keep.tile([P, HALF], U32, name="h_q_first", tag="b5", align_bytes=64)
+                second_stage(hb_first, codes, 0, HALF)
+            if c >= PER_HALF:
+                codes = ring.tile([P, CHUNK], U32, name="h_q", align_bytes=64)
+                second_stage(hbs[c], codes, c * CHUNK, CHUNK)

@@ -1,6 +1,7 @@
 from contextlib import ExitStack
 
 import concourse.mybir as mybir
+from concourse.masks import make_identity
 
 K, H, N, T, S = 1024, 512, 384, 4096, 1024
 FLOPS = 2 * (4 * K * H * S + H * N * S)
@@ -19,10 +20,8 @@ ALU = mybir.AluOpType
 P = 128
 PACK = 4
 PASSES = K // (P * PACK)
-HALF = 512
 CHUNK = 128
 CHUNKS = S // CHUNK
-PER_HALF = HALF // CHUNK
 N_TILES = N // P
 
 
@@ -39,92 +38,78 @@ def tile_list_synapse_direction_evidence_kernel(
         idx = [lists.tile([P, S // 16], U16, name="idx%d" % l) for l in range(2)]
         nc.sync.dma_start(idx[0][:], offs)
 
-        bw_sc_raw = keep.tile([P, PASSES, H], U8, name="bw_sc_raw", align_bytes=64)
-        nc.vector.memset(bw_sc_raw[:].bitcast(I32), 0)
+        bw_sc = keep.tile([P, PASSES, H], U8, name="bw_sc", align_bytes=64)
+        nc.vector.memset(bw_sc[:].bitcast(I32), 0)
 
-        tab_sc = keep.tile([P, T], U8, name="tab_sc", tag="table", align_bytes=64)
+        tab_sc = keep.tile([P, T], U8, name="tab_sc", tag="tab_sc", align_bytes=64)
         for q in range(4):
             nc.sync.dma_start(
                 tab_sc[32 * q + 24 : 32 * q + 32, :].bitcast(I32), tab_scales[:, 4 * q : 4 * q + 4, :].bitcast(I32)
             )
             nc.vector.memset(tab_sc[32 * q : 32 * q + 24, :].bitcast(I32), 0)
-        nc.sync.dma_start(idx[1][:], offs2)
 
+        tab_w = [keep.tile([P, T], U16, name="tab_w%d" % a, align_bytes=64) for a in range(PASSES)]
         aw_raw = [keep.tile([P, PACK, H], F32, name="aw_raw%d" % a, align_bytes=64) for a in range(PASSES)]
-
-        def load_aw(a):
+        bw_q = keep.tile([P, PASSES, H], I32, name="bw_q", align_bytes=64)
+        nc.sync.dma_start(tab_w[0][:].bitcast(I32), tab_words[0].bitcast(I32))
+        nc.sync.dma_start(bw_q[:], bw_words.rearrange("a p c i -> p a (c i)").bitcast(I32))
+        nc.sync.dma_start(tab_w[1][:].bitcast(I32), tab_words[1].bitcast(I32))
+        for q in range(4):
+            nc.sync.dma_start(
+                bw_sc[32 * q : 32 * q + 4].bitcast(I32),
+                bw_scales[:, 4 * q : 4 * q + 4, :].rearrange("a r c -> r a c").bitcast(I32),
+            )
+        for a in range(PASSES):
             nc.sync.dma_start(
                 aw_raw[a][:], aw[512 * a : 512 * (a + 1), :].rearrange("(p i) c -> p i c", i=PACK)
             )
-
-        load_aw(0)
-        bw_raw = keep.tile([P, PASSES, H], I32, name="bw_raw", align_bytes=64)
-        nc.sync.dma_start(bw_raw[:], bw_words.rearrange("a p c i -> p a (c i)").bitcast(I32))
-        for q in range(4):
-            nc.sync.dma_start(
-                bw_sc_raw[32 * q : 32 * q + 4].bitcast(I32),
-                bw_scales[:, 4 * q : 4 * q + 4, :].rearrange("a r c -> r a c").bitcast(I32),
-            )
-        tab_w = [keep.tile([P, T], U16, name="tab_w0", align_bytes=64)]
-        nc.sync.dma_start(tab_w[0][:].bitcast(I32), tab_words[0].bitcast(I32))
-        load_aw(1)
+            if a == 0:
+                nc.sync.dma_start(idx[1][:], offs2)
         gain_sb = keep.tile([P, PACK], F32, name="gain_sb", align_bytes=64)
         nc.sync.dma_start(gain_sb[:], gain.rearrange("(p t) -> p t", t=PACK))
 
-        v_sc = []
-        for a in range(PASSES):
-            v_sc.append(keep.tile([P, 2 * S], U8, name="v_sc%d" % a, align_bytes=64))
-            nc.gpsimd.memset(v_sc[a][96:128, :].bitcast(I32), 0)
+        v_sc = {}
+        for l in range(2):
+            for a in range(PASSES):
+                v_sc[a, l] = keep.tile([P, S], U8, name="v_sc%d_%d" % (a, l), align_bytes=64)
+                nc.gpsimd.memset(v_sc[a, l][96:128, :].bitcast(I32), 0)
+        ident = keep.tile([P, P], F32, name="ident", align_bytes=64)
+        make_identity(nc, ident[:])
 
         warm_in = keep.tile([P, 1], F32, name="warm_in")
         warm_out = keep.tile([P, 1], F32, name="warm_out")
         nc.vector.memset(warm_in[:], 0.0)
         nc.scalar.activation(warm_out[:], warm_in[:], ACT.Tanh)
 
-        both = keep.tile([P, 2 * S], U8, name="v_sc_both", tag="both", align_bytes=64)
-        for l in range(2):
-            nc.vector.tensor_copy(both[:, l * S : (l + 1) * S], tab_sc[:].indirect(idx[l][:]))
-        nc.sync.dma_start(v_sc[0][0:100, :].bitcast(I32), both[24:124, :].bitcast(I32))
-        tab_w.append(keep.tile([P, T], U16, name="tab_w1", tag="table", align_bytes=64))
-        nc.sync.dma_start(tab_w[1][:].bitcast(I32), tab_words[1].bitcast(I32))
-        nc.sync.dma_start(v_sc[1][0:100, :].bitcast(I32), both[28:128, :].bitcast(I32))
-
-        bw_q = keep.tile([P, PASSES, H], I32, name="bw_q", align_bytes=64)
-        nc.vector.tensor_copy(
-            bw_q[:].rearrange("p a (t c i) -> p a c t i", t=4, i=4),
-            bw_raw[:].rearrange("p a (c i t) -> p a c t i", t=4, i=4),
-        )
-        bw_sc = keep.tile([P, PASSES, H], U8, name="bw_sc", align_bytes=64)
-        nc.vector.tensor_copy(
-            bw_sc[:].rearrange("p a (t m) -> p a t m", t=4),
-            bw_sc_raw[:].rearrange("p a (m t) -> p a t m", t=4),
-        )
-
         v_w = {}
-
-        def gather_words(a, l, h, tag):
-            words = keep.tile([P, HALF], U16, name="v_w%d_%d_%d" % (a, l, h), tag=tag, align_bytes=64)
-            offsets = idx[l][:, h * (HALF // 16) : (h + 1) * (HALF // 16)]
-            nc.vector.tensor_copy(words[:], tab_w[a][:].indirect(offsets))
-            v_w[a, l, h] = words
+        for l in range(2):
+            both = keep.tile([P, S], U8, name="v_sc_both", tag="both", align_bytes=64)
+            nc.vector.tensor_copy(both[:], tab_sc[:].indirect(idx[l][:]))
+            for a in range(PASSES):
+                first = 24 + 4 * a
+                (nc.scalar, nc.sync)[l].dma_start(
+                    v_sc[a, l][0:100, :].bitcast(I32), both[first : first + 100, :].bitcast(I32)
+                )
+            for a in range(PASSES):
+                v_w[a, l] = keep.tile([P, S], U16, name="v_w%d_%d" % (a, l), align_bytes=64)
+                nc.vector.tensor_copy(v_w[a, l][:], tab_w[a][:].indirect(idx[l][:]))
 
         weights = {}
         for a in range(PASSES):
-            grouped = keep.tile([P, PACK * H], BF16, name="aw_bf%d" % a, tag="aw_bf%d" % a, align_bytes=64)
-            nc.scalar.copy(
-                grouped[:].rearrange("p (t m i) -> p m t i", t=4, i=4),
-                aw_raw[a][:].rearrange("p i (m t) -> p m t i", t=4),
-            )
-            for l in range(2):
-                gather_words(a, l, 0, "v_w%d_%d_0" % (a, l))
+            grouped = keep.tile([P, PACK * H], BF16, name="aw_bf%d" % a, align_bytes=64)
+            dst = grouped[:].rearrange("p (c n i) -> p c i n", n=4, i=4)
+            src = aw_raw[a][:].rearrange("p i (c n) -> p c i n", n=4)
+            if a == 0:
+                nc.scalar.copy(dst, src)
+            else:
+                nc.vector.tensor_copy(dst, src)
             codes = keep.tile([P, H], U32, name="aw_q%d" % a, align_bytes=64)
             scales = keep.tile([P, H], U8, name="aw_sc%d" % a, align_bytes=64)
             nc.vector.quantize_mx(out=codes[:].bitcast(FP8X4), scales=scales[:], in_=grouped[:])
             weights["a", a] = (codes[:], scales[:])
             weights["b", a] = (bw_q[:, a, :], bw_sc[:, a, :])
-        gather_words(0, 0, 1, "aw_bf1")
 
-        dw_w = keep.tile([P, 2 * N], U8, name="dw_w", tag="aw_bf0", align_bytes=64)
+        dw_w = keep.tile([P, 2 * N], U8, name="dw_w", tag="tab_sc", align_bytes=64)
         nc.sync.dma_start(dw_w[:].bitcast(I32), dw_words[0].bitcast(I32))
         dw_sc = keep.tile([P, N], U8, name="dw_sc", tag="both", align_bytes=64)
         nc.vector.memset(dw_sc[:].bitcast(I32), 0)
@@ -133,108 +118,98 @@ def tile_list_synapse_direction_evidence_kernel(
                 dw_sc[32 * q : 32 * q + 4, :].bitcast(I32), dw_scales[0, 4 * q : 4 * q + 4, :].bitcast(I32)
             )
 
-        def passes(bank, role, l, c, a):
+        def first_stage_pass(bank, role, l, c, a):
             codes, scales = weights[role, a]
-            h, c0 = divmod(c * CHUNK, HALF)
-            j0 = l * S + c * CHUNK
-            for t in range(PACK):
-                nc.tensor.matmul_mx(
-                    out=bank[:, t, :],
-                    lhsT=codes[:, t * P : (t + 1) * P].bitcast(FP8X4),
-                    lhsT_scale=scales[:, t * P : (t + 1) * P],
-                    rhs=v_w[a, l, h][:, c0 : c0 + CHUNK].bitcast(FP4X4),
-                    rhs_scale=v_sc[a][:, j0 : j0 + CHUNK],
-                    start=(a == 0 and t == 0),
-                    stop=(a == PASSES - 1 and t == PACK - 1),
-                )
+            j0 = c * CHUNK
+            nc.tensor.matmul_mx(
+                out=bank[:],
+                lhsT=v_w[a, l][:, j0 : j0 + CHUNK].bitcast(FP4X4),
+                lhsT_scale=v_sc[a, l][:, j0 : j0 + CHUNK],
+                rhs=codes.bitcast(FP8X4),
+                rhs_scale=scales,
+                start=(a == 0),
+                stop=(a == PASSES - 1),
+            )
 
-        products = [("b", 0), ("a", 0), ("b", 1), ("a", 1)]
-        banks = {}
+        def by_slice(bank):
+            return bank[:].rearrange("j (m t) -> j t m", t=PACK)
 
-        def open_chunk(c):
-            for role, l in products:
-                banks[role, l, c] = psum.tile([P, PACK, CHUNK], F32, name="bank", tag="bank")
-                passes(banks[role, l, c], role, l, c, 0)
+        b_vals = [keep.tile([P, 2, PACK, P], F32, name="b%d" % c, align_bytes=64) for c in range(CHUNKS)]
+
+        def keep_b(bank, l, c):
+            nc.scalar.activation(b_vals[c][:, l], by_slice(bank), ACT.Copy, scale=(-1.0, 1.0)[l])
+
+        for l in range(2):
+            banks = []
+            for c in range(CHUNKS):
+                banks.append(psum.tile([P, H], F32, name="bank", tag="bank"))
+                first_stage_pass(banks[c], "b", l, c, 0)
+            for c in range(CHUNKS):
+                first_stage_pass(banks[c], "b", l, c, 1)
+                keep_b(banks[c], l, c)
 
         def cross_products(c):
-            b_vals = keep.tile([P, 2, CHUNK, PACK], F32, name="b%d" % c, tag="b%d" % c, align_bytes=64)
-            for role, l in products:
-                if (role, l, c) not in banks:
-                    banks[role, l, c] = psum.tile([P, PACK, CHUNK], F32, name="bank", tag="bank")
-                    passes(banks[role, l, c], role, l, c, 0)
-                passes(banks[role, l, c], role, l, c, 1)
-                if role == "b":
-                    nc.scalar.copy(b_vals[:, l], banks[role, l, c][:].rearrange("p t j -> p j t"))
             prods = []
             for l in range(2):
-                prod = ring.tile([P, CHUNK, PACK], F32, name="prod%d" % l, align_bytes=64)
-                nc.vector.tensor_tensor(
-                    prod[:], banks["a", l, c][:].rearrange("p t j -> p j t"), b_vals[:, 1 - l], ALU.mult
-                )
+                bank = psum.tile([P, H], F32, name="bank", tag="bank")
+                for a in range(PASSES):
+                    first_stage_pass(bank, "a", l, c, a)
+                prod = ring.tile([P, PACK, P], F32, name="prod%d" % l, align_bytes=64)
+                nc.vector.tensor_tensor(prod[:], by_slice(bank), b_vals[c][:, 1 - l], ALU.mult)
                 prods.append(prod)
             return prods
 
-        def squash(prods, engine):
-            diff = ring.tile([P, CHUNK, PACK], F32, name="diff", align_bytes=64)
-            engine.tensor_tensor(diff[:], prods[0][:], prods[1][:], ALU.subtract)
+        def squash(prods):
+            bank = psum.tile([P, PACK, CHUNK], F32, name="bank", tag="bank")
+            for t in range(PACK):
+                for n, prod in enumerate(prods):
+                    nc.tensor.matmul(
+                        bank[:, t, :], prod[:, t, :], ident[:],
+                        start=(n == 0), stop=(n == len(prods) - 1), is_transpose=True,
+                    )
             th = ring.tile([P, CHUNK, PACK], F32, name="th", align_bytes=64)
-            nc.scalar.activation(th[:], diff[:], ACT.Tanh)
+            nc.scalar.activation(th[:], bank[:].rearrange("p t j -> p j t"), ACT.Tanh)
             return th
 
-        def scale(hb, th, engine):
-            engine.tensor_tensor(hb, th[:], gain_sb[:].unsqueeze(1).to_broadcast([P, CHUNK, PACK]), ALU.mult)
+        def scale(th):
+            hb = ring.tile([P, CHUNK, PACK], BF16, name="hb", align_bytes=64)
+            nc.vector.tensor_tensor(
+                hb[:], th[:], gain_sb[:].unsqueeze(1).to_broadcast([P, CHUNK, PACK]), ALU.mult
+            )
+            return hb
 
         out_v = out.rearrange("(c p) j -> p c j", p=P)
 
-        def second_stage(hb, codes, j0, width):
-            scales = ring.tile([P, width], U8, name="h_sc", align_bytes=64)
+        def second_stage(hb, c):
+            codes = ring.tile([P, CHUNK], U32, name="h_q", align_bytes=64)
+            scales = ring.tile([P, CHUNK], U8, name="h_sc", align_bytes=64)
             nc.vector.quantize_mx(
                 out=codes[:].bitcast(FP8X4), scales=scales[:], in_=hb[:].rearrange("p j t -> p (j t)")
             )
-            res = ring.tile([P, N_TILES, width], F32, name="res", align_bytes=64)
-            for c0 in range(0, width, CHUNK):
-                bank = psum.tile([P, N_TILES, CHUNK], F32, name="bank", tag="bank")
-                for n in range(N_TILES):
-                    nc.tensor.matmul_mx(
-                        out=bank[:, n, :],
-                        lhsT=dw_w[:, 2 * P * n : 2 * P * (n + 1)].bitcast(FP4X4),
-                        lhsT_scale=dw_sc[:, P * n : P * (n + 1)],
-                        rhs=codes[:, c0 : c0 + CHUNK].bitcast(FP8X4),
-                        rhs_scale=scales[:, c0 : c0 + CHUNK],
-                        start=True,
-                        stop=True,
-                    )
-                nc.scalar.copy(res[:, :, c0 : c0 + CHUNK], bank[:])
-            nc.sync.dma_start(out_v[:, :, j0 : j0 + width], res[:])
+            bank = psum.tile([P, N_TILES, CHUNK], F32, name="bank", tag="bank")
+            for n in range(N_TILES):
+                nc.tensor.matmul_mx(
+                    out=bank[:, n, :],
+                    lhsT=dw_w[:, 2 * P * n : 2 * P * (n + 1)].bitcast(FP4X4),
+                    lhsT_scale=dw_sc[:, P * n : P * (n + 1)],
+                    rhs=codes[:].bitcast(FP8X4),
+                    rhs_scale=scales[:],
+                    start=True,
+                    stop=True,
+                )
+            res = ring.tile([P, N_TILES, CHUNK], F32, name="res", align_bytes=64)
+            nc.scalar.copy(res[:], bank[:])
+            nc.sync.dma_start(out_v[:, :, c * CHUNK : (c + 1) * CHUNK], res[:])
 
-        late = [(0, 1), (1, 0), (1, 1)]
-        hb_first = keep.tile([P, HALF, PACK], BF16, name="hb_first", align_bytes=64)
+        prods = {}
         ths = {}
         hbs = {}
-        open_chunk(0)
-        open_chunk(1)
         for step in range(CHUNKS + 3):
             if step < CHUNKS:
-                prods = cross_products(step)
-            if step < PER_HALF:
-                ths[step] = squash(prods, nc.gpsimd)
-            if step < len(late):
-                gather_words(late[step][0], late[step][1], 1, "b%d" % step)
-            c = step - 1
-            if 0 <= c < PER_HALF - 1:
-                scale(hb_first[:, c * CHUNK : (c + 1) * CHUNK, :], ths[c], nc.gpsimd)
-            c = step - 2
-            if c == PER_HALF - 1:
-                scale(hb_first[:, c * CHUNK : (c + 1) * CHUNK, :], ths[c], nc.vector)
-            if PER_HALF <= c < CHUNKS:
-                hbs[c] = ring.tile([P, CHUNK, PACK], BF16, name="hb", align_bytes=64)
-                scale(hbs[c][:], ths[c], nc.vector)
-            if PER_HALF <= step < CHUNKS:
-                ths[step] = squash(prods, nc.vector)
-            c = step - 3
-            if c == PER_HALF - 1:
-                codes = keep.tile([P, HALF], U32, name="h_q_first", tag="b5", align_bytes=64)
-                second_stage(hb_first, codes, 0, HALF)
-            if c >= PER_HALF:
-                codes = ring.tile([P, CHUNK], U32, name="h_q", align_bytes=64)
-                second_stage(hbs[c], codes, c * CHUNK, CHUNK)
+                prods[step] = cross_products(step)
+            if 1 <= step < CHUNKS + 1:
+                ths[step - 1] = squash(prods[step - 1])
+            if 2 <= step < CHUNKS + 2:
+                hbs[step - 2] = scale(ths[step - 2])
+            if step >= 3:
+                second_stage(hbs[step - 3], step - 3)

@@ -19,10 +19,21 @@ ALU = mybir.AluOpType
 
 P = 128
 PACK = 4
-PASSES = K // (P * PACK)
+K_PASS = P * PACK
+PASSES = K // K_PASS
+PRE, POST = 0, 1
+SIDES = (PRE, POST)
 CHUNK = 128
 CHUNKS = S // CHUNK
 N_TILES = N // P
+QUADRANT = 32
+QUADRANTS = P // QUADRANT
+ROWS = 4
+TABLE_ROW0 = QUADRANT - PASSES * ROWS
+PLANE_SPAN = (QUADRANTS - 1) * QUADRANT + ROWS
+RING_BUFS = 4
+PSUM_BANKS = 8
+ALIGN = 64
 
 
 def tile_list_synapse_direction_evidence_kernel(
@@ -32,99 +43,110 @@ def tile_list_synapse_direction_evidence_kernel(
     with ExitStack() as ctx:
         lists = ctx.enter_context(tc.tile_pool(name="lists", bufs=1))
         keep = ctx.enter_context(tc.tile_pool(name="keep", bufs=1))
-        ring = ctx.enter_context(tc.tile_pool(name="ring", bufs=4))
-        psum = ctx.enter_context(tc.psum_pool(name="psum", bufs=8))
+        ring = ctx.enter_context(tc.tile_pool(name="ring", bufs=RING_BUFS))
+        shared = ctx.enter_context(tc.tile_pool(name="shared", bufs=1))
+        psum = ctx.enter_context(tc.psum_pool(name="psum", bufs=PSUM_BANKS))
 
-        idx = [lists.tile([P, S // 16], U16, name="idx%d" % l) for l in range(2)]
-        nc.sync.dma_start(idx[0][:], offs)
+        idx = [lists.tile([P, S // 16], U16, name="idx%d" % side) for side in SIDES]
+        nc.sync.dma_start(idx[PRE][:], offs)
 
-        bw_sc = keep.tile([P, PASSES, H], U8, name="bw_sc", align_bytes=64)
+        gain_sb = keep.tile([P, PACK], F32, name="gain_sb", align_bytes=ALIGN)
+        nc.sync.dma_start(gain_sb[:], gain.rearrange("(p t) -> p t", t=PACK))
+        gain_rep = keep.tile([P, CHUNK, PACK], F32, name="gain_rep", align_bytes=ALIGN)
+        nc.scalar.activation(gain_rep[:], gain_sb[:].unsqueeze(1).to_broadcast([P, CHUNK, PACK]), ACT.Copy)
+
+        bw_sc = keep.tile([P, PASSES, H], U8, name="bw_sc", align_bytes=ALIGN)
         nc.vector.memset(bw_sc[:].bitcast(I32), 0)
 
-        tab_sc = keep.tile([P, T], U8, name="tab_sc", tag="tab_sc", align_bytes=64)
-        for q in range(4):
+        tab_sc = keep.tile([P, T], U8, name="tab_sc", tag="tab_sc", align_bytes=ALIGN)
+        for q in range(QUADRANTS):
+            p0 = QUADRANT * q
             nc.sync.dma_start(
-                tab_sc[32 * q + 24 : 32 * q + 32, :].bitcast(I32), tab_scales[:, 4 * q : 4 * q + 4, :].bitcast(I32)
+                tab_sc[p0 + TABLE_ROW0 : p0 + QUADRANT, :].bitcast(I32),
+                tab_scales[:, ROWS * q : ROWS * (q + 1), :].bitcast(I32),
             )
-            nc.vector.memset(tab_sc[32 * q : 32 * q + 24, :].bitcast(I32), 0)
+            nc.vector.memset(tab_sc[p0 : p0 + TABLE_ROW0, :].bitcast(I32), 0)
+        nc.sync.dma_start(idx[POST][:], offs2)
 
-        tab_w = [keep.tile([P, T], U16, name="tab_w%d" % a, align_bytes=64) for a in range(PASSES)]
-        aw_raw = [keep.tile([P, PACK, H], F32, name="aw_raw%d" % a, align_bytes=64) for a in range(PASSES)]
-        bw_q = keep.tile([P, PASSES, H], I32, name="bw_q", align_bytes=64)
+        tab_w = [keep.tile([P, T], U16, name="tab_w%d" % a, align_bytes=ALIGN) for a in range(PASSES)]
+        bw_q = keep.tile([P, PASSES, H], I32, name="bw_q", align_bytes=ALIGN)
         nc.sync.dma_start(tab_w[0][:].bitcast(I32), tab_words[0].bitcast(I32))
         nc.sync.dma_start(bw_q[:], bw_words.rearrange("a p c i -> p a (c i)").bitcast(I32))
         nc.sync.dma_start(tab_w[1][:].bitcast(I32), tab_words[1].bitcast(I32))
-        for q in range(4):
+        for q in range(QUADRANTS):
             nc.sync.dma_start(
-                bw_sc[32 * q : 32 * q + 4].bitcast(I32),
-                bw_scales[:, 4 * q : 4 * q + 4, :].rearrange("a r c -> r a c").bitcast(I32),
+                bw_sc[QUADRANT * q : QUADRANT * q + ROWS].bitcast(I32),
+                bw_scales[:, ROWS * q : ROWS * (q + 1), :].rearrange("a r c -> r a c").bitcast(I32),
             )
-        for a in range(PASSES):
-            nc.sync.dma_start(
-                aw_raw[a][:], aw[512 * a : 512 * (a + 1), :].rearrange("(p i) c -> p i c", i=PACK)
-            )
-            if a == 0:
-                nc.sync.dma_start(idx[1][:], offs2)
-        gain_sb = keep.tile([P, PACK], F32, name="gain_sb", align_bytes=64)
-        nc.sync.dma_start(gain_sb[:], gain.rearrange("(p t) -> p t", t=PACK))
+
+        def load_aw(raw, a):
+            nc.sync.dma_start(raw[:], aw[K_PASS * a : K_PASS * (a + 1), :].rearrange("(p i) c -> p i c", i=PACK))
+            return raw
+
+        aw_raw = [load_aw(keep.tile([P, PACK, H], F32, name="aw_raw0", align_bytes=ALIGN), 0)]
 
         v_sc = {}
-        for l in range(2):
+        for side in SIDES:
             for a in range(PASSES):
-                v_sc[a, l] = keep.tile([P, S], U8, name="v_sc%d_%d" % (a, l), align_bytes=64)
-                nc.gpsimd.memset(v_sc[a, l][96:128, :].bitcast(I32), 0)
-        ident = keep.tile([P, P], F32, name="ident", align_bytes=64)
+                v_sc[a, side] = keep.tile([P, S], U8, name="v_sc%d_%d" % (a, side), align_bytes=ALIGN)
+                nc.gpsimd.memset(v_sc[a, side][P - QUADRANT : P, :].bitcast(I32), 0)
+        ident = keep.tile([P, P], F32, name="ident", align_bytes=ALIGN)
         make_identity(nc, ident[:])
 
-        warm_in = keep.tile([P, 1], F32, name="warm_in")
-        warm_out = keep.tile([P, 1], F32, name="warm_out")
-        nc.vector.memset(warm_in[:], 0.0)
-        nc.scalar.activation(warm_out[:], warm_in[:], ACT.Tanh)
+        def gather_scales(picked, side, queue):
+            nc.vector.tensor_copy(picked[:], tab_sc[:].indirect(idx[side][:]))
+            for a in range(PASSES):
+                first = TABLE_ROW0 + ROWS * a
+                queue.dma_start(
+                    v_sc[a, side][0:PLANE_SPAN, :].bitcast(I32), picked[first : first + PLANE_SPAN, :].bitcast(I32)
+                )
 
         v_w = {}
-        for l in range(2):
-            both = keep.tile([P, S], U8, name="v_sc_both", tag="both", align_bytes=64)
-            nc.vector.tensor_copy(both[:], tab_sc[:].indirect(idx[l][:]))
-            for a in range(PASSES):
-                first = 24 + 4 * a
-                (nc.scalar, nc.sync)[l].dma_start(
-                    v_sc[a, l][0:100, :].bitcast(I32), both[first : first + 100, :].bitcast(I32)
-                )
-            for a in range(PASSES):
-                v_w[a, l] = keep.tile([P, S], U16, name="v_w%d_%d" % (a, l), align_bytes=64)
-                nc.vector.tensor_copy(v_w[a, l][:], tab_w[a][:].indirect(idx[l][:]))
+
+        def gather_words(words, a, side):
+            nc.vector.tensor_copy(words[:], tab_w[a][:].indirect(idx[side][:]))
+            v_w[a, side] = words
+
+        aw_bytes = 4 * PACK * H
+        picked_pre = shared.tile([P, S], U8, name="picked_pre", align_bytes=ALIGN, offset=aw_bytes - S // 2)
+        gather_scales(picked_pre, PRE, nc.scalar)
+        aw_raw.append(load_aw(shared.tile([P, PACK, H], F32, name="aw_raw1", align_bytes=ALIGN, offset=0), 1))
+        gather_words(keep.tile([P, S], U16, name="v_w0_pre", align_bytes=ALIGN), 0, PRE)
+        gather_scales(keep.tile([P, S], U8, name="picked_post", tag="picked_post", align_bytes=ALIGN), POST, nc.sync)
+        gather_words(keep.tile([P, S], U16, name="v_w1_pre", align_bytes=ALIGN), 1, PRE)
+        gather_words(shared.tile([P, S], U16, name="v_w0_post", align_bytes=ALIGN, offset=aw_bytes), 0, POST)
+        gather_words(keep.tile([P, S], U16, name="v_w1_post", align_bytes=ALIGN), 1, POST)
 
         weights = {}
-        for a in range(PASSES):
-            grouped = keep.tile([P, PACK * H], BF16, name="aw_bf%d" % a, align_bytes=64)
-            dst = grouped[:].rearrange("p (c n i) -> p c i n", n=4, i=4)
-            src = aw_raw[a][:].rearrange("p i (c n) -> p c i n", n=4)
-            if a == 0:
-                nc.scalar.copy(dst, src)
-            else:
-                nc.vector.tensor_copy(dst, src)
-            codes = keep.tile([P, H], U32, name="aw_q%d" % a, align_bytes=64)
-            scales = keep.tile([P, H], U8, name="aw_sc%d" % a, align_bytes=64)
+        for a, round_copy in enumerate((nc.scalar.copy, nc.vector.tensor_copy)):
+            grouped = keep.tile([P, PACK * H], BF16, name="aw_bf%d" % a, align_bytes=ALIGN)
+            round_copy(
+                grouped[:].rearrange("p (c n i) -> p c i n", n=4, i=PACK),
+                aw_raw[a][:].rearrange("p i (c n) -> p c i n", n=4),
+            )
+            codes = keep.tile([P, H], U32, name="aw_q%d" % a, align_bytes=ALIGN)
+            scales = keep.tile([P, H], U8, name="aw_sc%d" % a, align_bytes=ALIGN)
             nc.vector.quantize_mx(out=codes[:].bitcast(FP8X4), scales=scales[:], in_=grouped[:])
             weights["a", a] = (codes[:], scales[:])
             weights["b", a] = (bw_q[:, a, :], bw_sc[:, a, :])
 
-        dw_w = keep.tile([P, 2 * N], U8, name="dw_w", tag="tab_sc", align_bytes=64)
+        dw_w = keep.tile([P, 2 * N], U8, name="dw_w", tag="tab_sc", align_bytes=ALIGN)
         nc.sync.dma_start(dw_w[:].bitcast(I32), dw_words[0].bitcast(I32))
-        dw_sc = keep.tile([P, N], U8, name="dw_sc", tag="both", align_bytes=64)
+        dw_sc = keep.tile([P, N], U8, name="dw_sc", tag="picked_post", align_bytes=ALIGN)
         nc.vector.memset(dw_sc[:].bitcast(I32), 0)
-        for q in range(4):
+        for q in range(QUADRANTS):
             nc.sync.dma_start(
-                dw_sc[32 * q : 32 * q + 4, :].bitcast(I32), dw_scales[0, 4 * q : 4 * q + 4, :].bitcast(I32)
+                dw_sc[QUADRANT * q : QUADRANT * q + ROWS, :].bitcast(I32),
+                dw_scales[0, ROWS * q : ROWS * (q + 1), :].bitcast(I32),
             )
 
-        def first_stage_pass(bank, role, l, c, a):
+        def first_stage_pass(bank, role, side, c, a):
             codes, scales = weights[role, a]
             j0 = c * CHUNK
             nc.tensor.matmul_mx(
                 out=bank[:],
-                lhsT=v_w[a, l][:, j0 : j0 + CHUNK].bitcast(FP4X4),
-                lhsT_scale=v_sc[a, l][:, j0 : j0 + CHUNK],
+                lhsT=v_w[a, side][:, j0 : j0 + CHUNK].bitcast(FP4X4),
+                lhsT_scale=v_sc[a, side][:, j0 : j0 + CHUNK],
                 rhs=codes.bitcast(FP8X4),
                 rhs_scale=scales,
                 start=(a == 0),
@@ -132,57 +154,56 @@ def tile_list_synapse_direction_evidence_kernel(
             )
 
         def by_slice(bank):
-            return bank[:].rearrange("j (m t) -> j t m", t=PACK)
+            return bank[:].rearrange("j (p t) -> j t p", t=PACK)
 
-        b_vals = [keep.tile([P, 2, PACK, P], F32, name="b%d" % c, align_bytes=64) for c in range(CHUNKS)]
-
-        def keep_b(bank, l, c):
-            nc.scalar.activation(b_vals[c][:, l], by_slice(bank), ACT.Copy, scale=(-1.0, 1.0)[l])
-
-        for l in range(2):
+        b_vals = [keep.tile([P, 2, PACK, P], F32, name="b%d" % c, align_bytes=ALIGN) for c in range(CHUNKS)]
+        b_sign = {PRE: -1.0, POST: 1.0}
+        for side in SIDES:
             banks = []
             for c in range(CHUNKS):
                 banks.append(psum.tile([P, H], F32, name="bank", tag="bank"))
-                first_stage_pass(banks[c], "b", l, c, 0)
+                first_stage_pass(banks[c], "b", side, c, 0)
             for c in range(CHUNKS):
-                first_stage_pass(banks[c], "b", l, c, 1)
-                keep_b(banks[c], l, c)
+                first_stage_pass(banks[c], "b", side, c, 1)
+                nc.scalar.activation(b_vals[c][:, side], by_slice(banks[c]), ACT.Copy, scale=b_sign[side])
 
         def cross_products(c):
             prods = []
-            for l in range(2):
+            for side in SIDES:
                 bank = psum.tile([P, H], F32, name="bank", tag="bank")
                 for a in range(PASSES):
-                    first_stage_pass(bank, "a", l, c, a)
-                prod = ring.tile([P, PACK, P], F32, name="prod%d" % l, align_bytes=64)
-                nc.vector.tensor_tensor(prod[:], by_slice(bank), b_vals[c][:, 1 - l], ALU.mult)
+                    first_stage_pass(bank, "a", side, c, a)
+                prod = ring.tile([P, PACK, P], F32, name="prod%d" % side, align_bytes=ALIGN)
+                nc.vector.tensor_tensor(prod[:], by_slice(bank), b_vals[c][:, 1 - side], ALU.mult)
                 prods.append(prod)
             return prods
 
         def squash(prods):
             bank = psum.tile([P, PACK, CHUNK], F32, name="bank", tag="bank")
             for t in range(PACK):
-                for n, prod in enumerate(prods):
+                for side in SIDES:
                     nc.tensor.matmul(
-                        bank[:, t, :], prod[:, t, :], ident[:],
-                        start=(n == 0), stop=(n == len(prods) - 1), is_transpose=True,
+                        bank[:, t, :],
+                        prods[side][:, t, :],
+                        ident[:],
+                        start=(side == PRE),
+                        stop=(side == POST),
+                        is_transpose=True,
                     )
-            th = ring.tile([P, CHUNK, PACK], F32, name="th", align_bytes=64)
+            th = ring.tile([P, CHUNK, PACK], F32, name="th", align_bytes=ALIGN)
             nc.scalar.activation(th[:], bank[:].rearrange("p t j -> p j t"), ACT.Tanh)
             return th
 
-        def scale(th):
-            hb = ring.tile([P, CHUNK, PACK], BF16, name="hb", align_bytes=64)
-            nc.vector.tensor_tensor(
-                hb[:], th[:], gain_sb[:].unsqueeze(1).to_broadcast([P, CHUNK, PACK]), ALU.mult
-            )
+        def apply_gain(th):
+            hb = ring.tile([P, CHUNK, PACK], BF16, name="hb", align_bytes=ALIGN)
+            nc.vector.tensor_tensor(hb[:], th[:], gain_rep[:], ALU.mult)
             return hb
 
-        out_v = out.rearrange("(c p) j -> p c j", p=P)
+        out_v = out.rearrange("(n p) j -> p n j", p=P)
 
         def second_stage(hb, c):
-            codes = ring.tile([P, CHUNK], U32, name="h_q", align_bytes=64)
-            scales = ring.tile([P, CHUNK], U8, name="h_sc", align_bytes=64)
+            codes = ring.tile([P, CHUNK], U32, name="h_q", align_bytes=ALIGN)
+            scales = ring.tile([P, CHUNK], U8, name="h_sc", align_bytes=ALIGN)
             nc.vector.quantize_mx(
                 out=codes[:].bitcast(FP8X4), scales=scales[:], in_=hb[:].rearrange("p j t -> p (j t)")
             )
@@ -197,7 +218,7 @@ def tile_list_synapse_direction_evidence_kernel(
                     start=True,
                     stop=True,
                 )
-            res = ring.tile([P, N_TILES, CHUNK], F32, name="res", align_bytes=64)
+            res = ring.tile([P, N_TILES, CHUNK], F32, name="res", align_bytes=ALIGN)
             nc.scalar.copy(res[:], bank[:])
             nc.sync.dma_start(out_v[:, :, c * CHUNK : (c + 1) * CHUNK], res[:])
 
@@ -210,6 +231,6 @@ def tile_list_synapse_direction_evidence_kernel(
             if 1 <= step < CHUNKS + 1:
                 ths[step - 1] = squash(prods[step - 1])
             if 2 <= step < CHUNKS + 2:
-                hbs[step - 2] = scale(ths[step - 2])
+                hbs[step - 2] = apply_gain(ths[step - 2])
             if step >= 3:
                 second_stage(hbs[step - 3], step - 3)

from contextlib import ExitStack

import concourse.mybir as mybir
from concourse.masks import make_identity

K, H, N, T, S = 1024, 512, 384, 4096, 1024
FLOPS = 2 * (4 * K * H * S + H * N * S)

F32 = mybir.dt.float32
BF16 = mybir.dt.bfloat16
I32 = mybir.dt.int32
U32 = mybir.dt.uint32
U16 = mybir.dt.uint16
U8 = mybir.dt.uint8
FP8X4 = mybir.dt.float8_e4m3fn_x4
FP4X4 = mybir.dt.float4_e2m1fn_x4
ACT = mybir.ActivationFunctionType
ALU = mybir.AluOpType

P = 128
PACK = 4
K_PASS = P * PACK
PASSES = K // K_PASS
PRE, POST = 0, 1
SIDES = (PRE, POST)
CHUNK = 128
CHUNKS = S // CHUNK
N_TILES = N // P
QUADRANT = 32
QUADRANTS = P // QUADRANT
ROWS = 4
TABLE_ROW0 = QUADRANT - PASSES * ROWS
PLANE_SPAN = (QUADRANTS - 1) * QUADRANT + ROWS
RING_BUFS = 4
PSUM_BANKS = 8
ALIGN = 64


def tile_list_synapse_direction_evidence_kernel(
    tc, tab_words, tab_scales, offs, offs2, aw, bw_words, bw_scales, gain, dw_words, dw_scales, out
):
    nc = tc.nc
    with ExitStack() as ctx:
        lists = ctx.enter_context(tc.tile_pool(name="lists", bufs=1))
        keep = ctx.enter_context(tc.tile_pool(name="keep", bufs=1))
        ring = ctx.enter_context(tc.tile_pool(name="ring", bufs=RING_BUFS))
        shared = ctx.enter_context(tc.tile_pool(name="shared", bufs=1))
        psum = ctx.enter_context(tc.psum_pool(name="psum", bufs=PSUM_BANKS))

        idx = [lists.tile([P, S // 16], U16, name="idx%d" % side) for side in SIDES]
        nc.sync.dma_start(idx[PRE][:], offs)

        gain_sb = keep.tile([P, PACK], F32, name="gain_sb", align_bytes=ALIGN)
        nc.sync.dma_start(gain_sb[:], gain.rearrange("(p t) -> p t", t=PACK))
        gain_rep = keep.tile([P, CHUNK, PACK], F32, name="gain_rep", align_bytes=ALIGN)
        nc.scalar.activation(gain_rep[:], gain_sb[:].unsqueeze(1).to_broadcast([P, CHUNK, PACK]), ACT.Copy)

        bw_sc = keep.tile([P, PASSES, H], U8, name="bw_sc", align_bytes=ALIGN)
        nc.vector.memset(bw_sc[:].bitcast(I32), 0)

        tab_sc = keep.tile([P, T], U8, name="tab_sc", tag="tab_sc", align_bytes=ALIGN)
        for q in range(QUADRANTS):
            p0 = QUADRANT * q
            nc.sync.dma_start(
                tab_sc[p0 + TABLE_ROW0 : p0 + QUADRANT, :].bitcast(I32),
                tab_scales[:, ROWS * q : ROWS * (q + 1), :].bitcast(I32),
            )
            nc.vector.memset(tab_sc[p0 : p0 + TABLE_ROW0, :].bitcast(I32), 0)
        nc.sync.dma_start(idx[POST][:], offs2)

        tab_w = [keep.tile([P, T], U16, name="tab_w%d" % a, align_bytes=ALIGN) for a in range(PASSES)]
        bw_q = keep.tile([P, PASSES, H], I32, name="bw_q", align_bytes=ALIGN)
        nc.sync.dma_start(tab_w[0][:].bitcast(I32), tab_words[0].bitcast(I32))
        nc.sync.dma_start(bw_q[:], bw_words.rearrange("a p c i -> p a (c i)").bitcast(I32))
        nc.sync.dma_start(tab_w[1][:].bitcast(I32), tab_words[1].bitcast(I32))
        for q in range(QUADRANTS):
            nc.sync.dma_start(
                bw_sc[QUADRANT * q : QUADRANT * q + ROWS].bitcast(I32),
                bw_scales[:, ROWS * q : ROWS * (q + 1), :].rearrange("a r c -> r a c").bitcast(I32),
            )

        def load_aw(raw, a):
            nc.sync.dma_start(raw[:], aw[K_PASS * a : K_PASS * (a + 1), :].rearrange("(p i) c -> p i c", i=PACK))
            return raw

        aw_raw = [load_aw(keep.tile([P, PACK, H], F32, name="aw_raw0", align_bytes=ALIGN), 0)]

        v_sc = {}
        for side in SIDES:
            for a in range(PASSES):
                v_sc[a, side] = keep.tile([P, S], U8, name="v_sc%d_%d" % (a, side), align_bytes=ALIGN)
                nc.gpsimd.memset(v_sc[a, side][P - QUADRANT : P, :].bitcast(I32), 0)
        ident = keep.tile([P, P], F32, name="ident", align_bytes=ALIGN)
        make_identity(nc, ident[:])

        def gather_scales(picked, side, queue):
            nc.vector.tensor_copy(picked[:], tab_sc[:].indirect(idx[side][:]))
            for a in range(PASSES):
                first = TABLE_ROW0 + ROWS * a
                queue.dma_start(
                    v_sc[a, side][0:PLANE_SPAN, :].bitcast(I32), picked[first : first + PLANE_SPAN, :].bitcast(I32)
                )

        v_w = {}

        def gather_words(words, a, side):
            nc.vector.tensor_copy(words[:], tab_w[a][:].indirect(idx[side][:]))
            v_w[a, side] = words

        aw_bytes = 4 * PACK * H
        picked_pre = shared.tile([P, S], U8, name="picked_pre", align_bytes=ALIGN, offset=aw_bytes - S // 2)
        gather_scales(picked_pre, PRE, nc.scalar)
        aw_raw.append(load_aw(shared.tile([P, PACK, H], F32, name="aw_raw1", align_bytes=ALIGN, offset=0), 1))
        gather_words(keep.tile([P, S], U16, name="v_w0_pre", align_bytes=ALIGN), 0, PRE)
        gather_scales(keep.tile([P, S], U8, name="picked_post", tag="picked_post", align_bytes=ALIGN), POST, nc.sync)
        gather_words(keep.tile([P, S], U16, name="v_w1_pre", align_bytes=ALIGN), 1, PRE)
        gather_words(shared.tile([P, S], U16, name="v_w0_post", align_bytes=ALIGN, offset=aw_bytes), 0, POST)
        gather_words(keep.tile([P, S], U16, name="v_w1_post", align_bytes=ALIGN), 1, POST)

        weights = {}
        for a, round_copy in enumerate((nc.scalar.copy, nc.vector.tensor_copy)):
            grouped = keep.tile([P, PACK * H], BF16, name="aw_bf%d" % a, align_bytes=ALIGN)
            round_copy(
                grouped[:].rearrange("p (c n i) -> p c i n", n=4, i=PACK),
                aw_raw[a][:].rearrange("p i (c n) -> p c i n", n=4),
            )
            codes = keep.tile([P, H], U32, name="aw_q%d" % a, align_bytes=ALIGN)
            scales = keep.tile([P, H], U8, name="aw_sc%d" % a, align_bytes=ALIGN)
            nc.vector.quantize_mx(out=codes[:].bitcast(FP8X4), scales=scales[:], in_=grouped[:])
            weights["a", a] = (codes[:], scales[:])
            weights["b", a] = (bw_q[:, a, :], bw_sc[:, a, :])

        dw_w = keep.tile([P, 2 * N], U8, name="dw_w", tag="tab_sc", align_bytes=ALIGN)
        nc.sync.dma_start(dw_w[:].bitcast(I32), dw_words[0].bitcast(I32))
        dw_sc = keep.tile([P, N], U8, name="dw_sc", tag="picked_post", align_bytes=ALIGN)
        nc.vector.memset(dw_sc[:].bitcast(I32), 0)
        for q in range(QUADRANTS):
            nc.sync.dma_start(
                dw_sc[QUADRANT * q : QUADRANT * q + ROWS, :].bitcast(I32),
                dw_scales[0, ROWS * q : ROWS * (q + 1), :].bitcast(I32),
            )

        def first_stage_pass(bank, role, side, c, a):
            codes, scales = weights[role, a]
            j0 = c * CHUNK
            nc.tensor.matmul_mx(
                out=bank[:],
                lhsT=v_w[a, side][:, j0 : j0 + CHUNK].bitcast(FP4X4),
                lhsT_scale=v_sc[a, side][:, j0 : j0 + CHUNK],
                rhs=codes.bitcast(FP8X4),
                rhs_scale=scales,
                start=(a == 0),
                stop=(a == PASSES - 1),
            )

        def by_slice(bank):
            return bank[:].rearrange("j (p t) -> j t p", t=PACK)

        b_vals = [keep.tile([P, 2, PACK, P], F32, name="b%d" % c, align_bytes=ALIGN) for c in range(CHUNKS)]
        b_sign = {PRE: -1.0, POST: 1.0}
        for side in SIDES:
            banks = []
            for c in range(CHUNKS):
                banks.append(psum.tile([P, H], F32, name="bank", tag="bank"))
                first_stage_pass(banks[c], "b", side, c, 0)
            for c in range(CHUNKS):
                first_stage_pass(banks[c], "b", side, c, 1)
                nc.scalar.activation(b_vals[c][:, side], by_slice(banks[c]), ACT.Copy, scale=b_sign[side])

        def cross_products(c):
            prods = []
            for side in SIDES:
                bank = psum.tile([P, H], F32, name="bank", tag="bank")
                for a in range(PASSES):
                    first_stage_pass(bank, "a", side, c, a)
                prod = ring.tile([P, PACK, P], F32, name="prod%d" % side, align_bytes=ALIGN)
                nc.vector.tensor_tensor(prod[:], by_slice(bank), b_vals[c][:, 1 - side], ALU.mult)
                prods.append(prod)
            return prods

        def squash(prods):
            bank = psum.tile([P, PACK, CHUNK], F32, name="bank", tag="bank")
            for t in range(PACK):
                for side in SIDES:
                    nc.tensor.matmul(
                        bank[:, t, :],
                        prods[side][:, t, :],
                        ident[:],
                        start=(side == PRE),
                        stop=(side == POST),
                        is_transpose=True,
                    )
            th = ring.tile([P, CHUNK, PACK], F32, name="th", align_bytes=ALIGN)
            nc.scalar.activation(th[:], bank[:].rearrange("p t j -> p j t"), ACT.Tanh)
            return th

        def apply_gain(th):
            hb = ring.tile([P, CHUNK, PACK], BF16, name="hb", align_bytes=ALIGN)
            nc.vector.tensor_tensor(hb[:], th[:], gain_rep[:], ALU.mult)
            return hb

        out_v = out.rearrange("(n p) j -> p n j", p=P)

        def second_stage(hb, c):
            codes = ring.tile([P, CHUNK], U32, name="h_q", align_bytes=ALIGN)
            scales = ring.tile([P, CHUNK], U8, name="h_sc", align_bytes=ALIGN)
            nc.vector.quantize_mx(
                out=codes[:].bitcast(FP8X4), scales=scales[:], in_=hb[:].rearrange("p j t -> p (j t)")
            )
            bank = psum.tile([P, N_TILES, CHUNK], F32, name="bank", tag="bank")
            for n in range(N_TILES):
                nc.tensor.matmul_mx(
                    out=bank[:, n, :],
                    lhsT=dw_w[:, 2 * P * n : 2 * P * (n + 1)].bitcast(FP4X4),
                    lhsT_scale=dw_sc[:, P * n : P * (n + 1)],
                    rhs=codes[:].bitcast(FP8X4),
                    rhs_scale=scales[:],
                    start=True,
                    stop=True,
                )
            res = ring.tile([P, N_TILES, CHUNK], F32, name="res", align_bytes=ALIGN)
            nc.scalar.copy(res[:], bank[:])
            nc.sync.dma_start(out_v[:, :, c * CHUNK : (c + 1) * CHUNK], res[:])

        prods = {}
        ths = {}
        hbs = {}
        for step in range(CHUNKS + 3):
            if step < CHUNKS:
                prods[step] = cross_products(step)
            if 1 <= step < CHUNKS + 1:
                ths[step - 1] = squash(prods[step - 1])
            if 2 <= step < CHUNKS + 2:
                hbs[step - 2] = apply_gain(ths[step - 2])
            if step >= 3:
                second_stage(hbs[step - 3], step - 3)
